import numpy as np
import ml_dtypes


def mxq(x, axis, fmt="e4m3"):
    dtype, down = {"e4m3": (ml_dtypes.float8_e4m3fn, 7), "e5m2": (ml_dtypes.float8_e5m2, 14)}[fmt]
    v = np.moveaxis(np.asarray(x, np.float32).astype(ml_dtypes.bfloat16).astype(np.float64), axis, -1)
    blocks = v.reshape(v.shape[:-1] + (-1, 32))
    amax = np.abs(blocks).max(-1, keepdims=True)
    byte = np.maximum(np.where(amax > 0, np.frexp(amax)[1] - 1 + 127, 0) - down, 1)
    scale = np.exp2(byte - 127.0)
    codes = (blocks / scale).astype(np.float32).astype(dtype).astype(np.float64)
    return np.moveaxis((codes * scale).reshape(v.shape), -1, axis)


WIDE = False


def mx_kscale(k):
    if not WIDE:
        return np.ones(k)
    levels = np.array([10, -10, 5, -5, 0])
    if k % 512:
        return np.exp2(np.random.permutation(np.resize(levels, k // 32))).repeat(32)
    a = np.empty((k // 512, 16))
    for p in range(k // 512):
        a[p, :8] = np.random.permutation(np.resize(levels, 8))
        for g in range(8):
            far = levels[np.abs(levels - a[p, g]) >= 10]
            a[p, g + 8] = far[np.random.randint(len(far))]
    return np.exp2(a.ravel()).repeat(32)


def f64(x):
    return np.asarray(x).astype(np.float64)


def striped(idx):
    return np.tile(np.asarray(idx).reshape(-1, 16).T, (8, 1)).astype(np.uint16)


def unstriped(offs):
    return offs[:16].T.reshape(-1).astype(np.int64)


E2M1 = np.array([0.0, 0.5, 1.0, 1.5, 2.0, 3.0, 4.0, 6.0, -0.0, -0.5, -1.0, -1.5, -2.0, -3.0, -4.0, -6.0])


def pack_weight(w, fmt):
    k, n = w.shape
    w = f64(np.asarray(w, np.float32).astype(ml_dtypes.bfloat16)).reshape(k // 32, 32, n)
    amax = np.abs(w).max(1)
    if fmt == "e4m3":
        byte = np.frexp(amax)[1] - 1 + 127 - 7
    else:
        mant, ex = np.frexp(amax / 6.0)
        byte = np.where(mant > 0.5, ex, ex - 1) + 127
    byte = np.clip(np.where(amax > 0, byte, 1), 1, 254)
    scaled = (w * np.exp2(127.0 - byte)[:, None, :]).reshape(k, n).astype(np.float32)
    by_word = np.ascontiguousarray(scaled.reshape(k // 512, 128, 4, n).transpose(0, 1, 3, 2))
    if fmt == "e4m3":
        words = by_word.astype(ml_dtypes.float8_e4m3fn).view(np.uint8)
    else:
        c = by_word.astype(ml_dtypes.float4_e2m1fn).view(np.uint8) & 0xF
        words = (c[..., 0::2] | (c[..., 1::2] << 4)).reshape(k // 512, 128, 2 * n)
    return np.ascontiguousarray(words), np.ascontiguousarray(byte.astype(np.uint8).reshape(k // 512, 16, n))


def unpack_weight(words, scales, fmt):
    g, _, n = scales.shape
    words = np.ascontiguousarray(words).reshape(g, 128, n, -1)
    if fmt == "e4m3":
        vals = words.view(ml_dtypes.float8_e4m3fn).astype(np.float64)
    else:
        nib = np.empty((g, 128, n, 4), np.uint8)
        nib[..., 0::2] = words & 0xF
        nib[..., 1::2] = words >> 4
        vals = E2M1[nib]
    vals = vals * np.repeat(np.exp2(scales.astype(np.float64) - 127.0), 8, axis=1)[..., None]
    return vals.transpose(0, 1, 3, 2).reshape(g * 512, n)


def softplus(v):
    return np.log(1.0 + np.exp(v))


B, N, T, D, NQ = 1, 512, 2048, 1024, 256
SEG = 32


def setup_inputs():
    n = np.random.standard_normal
    idx = np.random.permutation(T)[:B * N]
    s = mx_kscale(D)[:, None]
    kp = pack_weight(n((D, T)) / s, "e2m1")
    return {
        "qT": (n((B, D, NQ)) * s * (1.00 / np.sqrt(D))).astype(np.float32),
        "k_words": np.ascontiguousarray(kp[0].reshape(1, 2, 128, T, 2).transpose(0, 2, 3, 1, 4)).reshape(1, 128, T, 4),
        "k_scales": kp[1],
        "lq": np.tile(np.random.uniform(-1.0, 1.0, 2048), (128, 1)).astype(np.float32),
        "offs": striped(idx),
    }


def reference(qT, k_words, k_scales, lq, offs):
    idx = unstriped(offs)
    pick = lambda x, which: x[:, which].reshape(x.shape[0], B, -1).transpose(1, 0, 2)
    k = unpack_weight(k_words.reshape(1, 128, T, 2, 2).transpose(0, 3, 1, 2, 4).reshape(2, 128, 2 * T), k_scales, "e2m1")
    kg = pick(k, idx)
    qq = mxq(f64(qT), 1, "e4m3")
    a = qq.transpose(0, 2, 1) @ kg
    y = softplus(a - pick(f64(lq), idx)[:, :1, :]).reshape(B, NQ, N // SEG, SEG).sum(-1)
    return y

@@ -1,0 +1,195 @@
+import math
+from contextlib import ExitStack
+
+import concourse.mybir as mybir
+from concourse.masks import make_identity
+
+F32 = mybir.dt.float32
+BF16 = mybir.dt.bfloat16
+I32 = mybir.dt.int32
+U32 = mybir.dt.uint32
+U16 = mybir.dt.uint16
+U8 = mybir.dt.uint8
+FP8X4 = mybir.dt.float8_e4m3fn_x4
+FP4X4 = mybir.dt.float4_e2m1fn_x4
+ACT = mybir.ActivationFunctionType
+ALU = mybir.AluOpType
+AXIS = mybir.AxisListType
+
+P = 128
+T = 2048
+N = 512
+D = 1024
+NQ = 256
+SEG = 32
+PASSES = 2
+PACK = 4
+TILES = N // P
+HALVES = NQ // P
+RUNS = N // SEG
+RUN_PART = SEG // TILES
+CAP = 11.0
+ROW = 12
+
+FLOPS = 2 * NQ * N * D
+BYTES = D * NQ * 4 + P * T * 4 + 2 * 16 * T + T * 4 + P * 32 * 2 + NQ * RUNS * 4
+
+
+def tile_attend_nce_topk_kernel(tc, qT, k_words, k_scales, lq, offs, out):
+    nc = tc.nc
+    with ExitStack() as ctx:
+        sb = ctx.enter_context(tc.tile_pool(name="sb", bufs=1))
+        ps = ctx.enter_context(tc.psum_pool(name="ps", bufs=1))
+
+        def bank(index, name):
+            return ps.tile([P, 512], F32, name=name, tag="bank%d" % index)
+
+        offsets = sb.tile([P, N // 16], U16, name="offsets")
+        nc.sync.dma_start(offsets[:], offs)
+
+        scale_pool = sb.tile([P, T], U8, name="scale_pool", align_bytes=64)
+        nc.sync.dma_start(
+            scale_pool[96:128, :].bitcast(I32), k_scales.rearrange("o f t -> f o t").bitcast(I32)
+        )
+        nc.vector.memset(scale_pool[0:96, :].bitcast(I32), 0)
+        lq_pool = sb.tile([P, T], F32, name="lq_pool", align_bytes=64)
+        nc.sync.dma_start(lq_pool[P - 1 : P, :], lq[0:1, :])
+        nc.vector.memset(lq_pool[0 : P - 1, :], 0.0)
+
+        word_pool = sb.tile([P, T], U32, name="word_pool", align_bytes=64)
+        nc.sync.dma_start(word_pool[:].bitcast(I32), k_words[0].rearrange("p t b -> p (t b)").bitcast(I32))
+        q_raw = []
+        for o in range(PASSES):
+            raw = sb.tile([P, PACK, NQ], F32, name="q_raw%d" % o, align_bytes=64)
+            nc.sync.dma_start(raw[:], qT[0, 512 * o : 512 * (o + 1), :].rearrange("(p t) w -> p t w", t=PACK))
+            q_raw.append(raw)
+
+        warm = sb.tile([P, 1], F32, name="warm")
+        nc.gpsimd.memset(warm[:], 0.0)
+        nc.scalar.activation(warm[:], warm[:], ACT.Exp)
+
+        ident = sb.tile([P, P], F32, name="ident", align_bytes=64)
+        make_identity(nc, ident[:])
+
+        k_scale = sb.tile([P, PASSES, N], U8, name="k_scale", align_bytes=64)
+        nc.gpsimd.memset(k_scale[:].rearrange("p o n -> p (o n)").bitcast(I32), 0)
+
+        scale_listed = sb.tile([P, N], U8, name="scale_listed", align_bytes=64)
+        nc.vector.tensor_copy(scale_listed[:], scale_pool[:].indirect(offsets[:]))
+        scale_dealt = sb.tile([P, N], U8, name="scale_dealt", align_bytes=64)
+        nc.vector.tensor_copy(
+            scale_dealt[:].bitcast(I32).rearrange("p (r j u) -> p r j u", r=TILES, j=RUNS),
+            scale_listed[:].bitcast(I32).rearrange("p (j r u) -> p r j u", r=TILES, j=RUNS),
+        )
+        for quad in range(4):
+            nc.scalar.dma_start(
+                k_scale[32 * quad : 32 * quad + 4].rearrange("p o n -> p (o n)").bitcast(I32),
+                scale_dealt[96 + 8 * quad : 96 + 8 * quad + 8, :].bitcast(I32),
+            )
+
+        lq_listed = sb.tile([P, N], F32, name="lq_listed", align_bytes=64)
+        nc.vector.tensor_copy(lq_listed[:], lq_pool[:].indirect(offsets[:]))
+        lq_dealt = sb.tile([P, N], F32, name="lq_dealt", align_bytes=64)
+        nc.scalar.copy(
+            lq_dealt[:].rearrange("p (r j u) -> p r j u", r=TILES, j=RUNS),
+            lq_listed[:].rearrange("p (j r u) -> p r j u", r=TILES, j=RUNS),
+        )
+        lq_turned = bank(7, "lq_turned")
+        for r in range(TILES):
+            nc.tensor.transpose(lq_turned[:, P * r : P * (r + 1)], lq_dealt[:, P * r : P * (r + 1)], ident[:])
+        minus_lq = sb.tile([P, TILES], F32, name="minus_lq")
+        minus_lq_cap = sb.tile([P, TILES], F32, name="minus_lq_cap")
+        lq_columns = lq_turned[:].rearrange("p (r x) -> p r x", r=TILES)[:, :, P - 1]
+        nc.scalar.activation(minus_lq[:], lq_columns, ACT.Copy, scale=-1.0)
+        nc.scalar.activation(minus_lq_cap[:], lq_columns, ACT.Copy, scale=-1.0, bias=-CAP)
+
+        word_listed = sb.tile([P, N], U32, name="word_listed", align_bytes=64)
+        nc.vector.tensor_copy(word_listed[:], word_pool[:].indirect(offsets[:]))
+        halves16 = word_listed[:].bitcast(U16).rearrange("p (j r u o) -> p o r j u", r=TILES, j=RUNS, o=PASSES)
+        k_codes = []
+        for o in range(PASSES):
+            codes = sb.tile([P, 2 * N], U8, name="k_codes%d" % o, align_bytes=64)
+            nc.vector.tensor_copy(
+                codes[:].bitcast(U16).rearrange("p (r j u) -> p r j u", r=TILES, j=RUNS), halves16[:, o]
+            )
+            k_codes.append(codes)
+
+        q_codes = {}
+        q_scale = {}
+        order = [(0, 0), (0, 1), (1, 1), (1, 0)]
+        for o, h in order:
+            woven = sb.tile([P, P, PACK], BF16, name="q_woven%d%d" % (o, h), align_bytes=64)
+            dst = woven[:].rearrange("p (c i) t -> p c t i", i=4)
+            src = q_raw[o][:, :, P * h : P * (h + 1)].rearrange("p t (c i) -> p c t i", i=4)
+            if (o, h) == (1, 1):
+                nc.vector.tensor_copy(dst, src)
+            else:
+                nc.scalar.copy(dst, src)
+            q_codes[o, h] = sb.tile([P, P], U32, name="q_codes%d%d" % (o, h), align_bytes=64)
+            q_scale[o, h] = sb.tile([P, P], U8, name="q_scale%d%d" % (o, h), align_bytes=64)
+            nc.vector.quantize_mx(
+                out=q_codes[o, h][:].bitcast(FP8X4),
+                scales=q_scale[o, h][:],
+                in_=woven[:].rearrange("p w t -> p (w t)"),
+            )
+
+        scores = {}
+        for h in range(HALVES):
+            for r in range(TILES):
+                scores[r, h] = bank(TILES * h + r, "scores%d%d" % (r, h))
+        for o, h in order:
+            for r in range(TILES):
+                nc.tensor.matmul_mx(
+                    out=scores[r, h][:, 0:P],
+                    lhsT=k_codes[o][:, 2 * P * r : 2 * P * (r + 1)].bitcast(FP4X4),
+                    lhsT_scale=k_scale[:, o, P * r : P * (r + 1)],
+                    rhs=q_codes[o, h][:].bitcast(FP8X4),
+                    rhs_scale=q_scale[o, h][:],
+                    start=(o == 0),
+                    stop=(o == PASSES - 1),
+                )
+
+        h_order = [1, 0]
+        expv = {}
+        over = {}
+        for h in h_order:
+            expv[h] = sb.tile([P, TILES, P], F32, name="expv%d" % h, align_bytes=64)
+            over[h] = sb.tile([P, TILES, P], F32, name="over%d" % h, align_bytes=64)
+            for r in range(TILES):
+                nc.scalar.activation(expv[h][:, r, :], scores[r, h][:, 0:P], ACT.Exp, bias=minus_lq[:, r : r + 1])
+        terms = sb.tile([P, HALVES, RUNS, ROW], F32, name="terms", align_bytes=64)
+        prod_turned = {}
+        for n, h in enumerate(h_order):
+            for r in range(TILES):
+                nc.vector.tensor_scalar(
+                    over[h][:, r, :], scores[r, h][:, 0:P], minus_lq_cap[:, r : r + 1], 0.0, ALU.add, ALU.max
+                )
+            grown = sb.tile([P, TILES, P], F32, name="grown%d" % h, align_bytes=64)
+            nc.vector.tensor_scalar(grown[:], expv[h][:], math.exp(CAP), 1.0, ALU.min, ALU.add)
+            pairs = sb.tile([P, 2, P], F32, name="pairs%d" % h, align_bytes=64)
+            nc.vector.tensor_tensor(pairs[:], grown[:, 0:2, :], grown[:, 2:4, :], ALU.mult)
+            quads = sb.tile([P, P], F32, name="quads%d" % h, align_bytes=64)
+            nc.vector.tensor_tensor(quads[:], pairs[:, 0, :], pairs[:, 1, :], ALU.mult)
+            over_sum = bank(TILES * h_order[0] + 2 * n, "over_sum%d" % h)
+            for r in range(TILES):
+                nc.tensor.matmul(
+                    over_sum[:, 0:P], over[h][:, r, :], ident[:],
+                    start=(r == 0), stop=(r == TILES - 1), is_transpose=True,
+                )
+            prod_turned[h] = bank(TILES * h_order[0] + 2 * n + 1, "prod_turned%d" % h)
+            nc.tensor.transpose(prod_turned[h][:, 0:P], quads[:], ident[:])
+            nc.vector.tensor_reduce(
+                terms[:, h, :, RUN_PART],
+                over_sum[:, 0:P].rearrange("p (j u) -> p j u", u=RUN_PART),
+                AXIS.X,
+                ALU.add,
+            )
+        result = sb.tile([P, HALVES, RUNS], F32, name="result", align_bytes=64)
+        for h in h_order:
+            nc.scalar.activation(
+                terms[:, h, :, 0:RUN_PART],
+                prod_turned[h][:, 0:P].rearrange("p (j u) -> p j u", u=RUN_PART),
+                ACT.Ln,
+            )
+            nc.vector.tensor_reduce(result[:, h, :], terms[:, h, :, 0 : RUN_PART + 1], AXIS.X, ALU.add)
+        nc.sync.dma_start(out[0].rearrange("(h p) j -> p h j", p=P), result[:])

@@ -47,32 +47,38 @@ def tile_attend_nce_topk_kernel(tc, qT, k_words, k_scales, lq, offs, out):
         offsets = sb.tile([P, N // 16], U16, name="offsets")
         nc.sync.dma_start(offsets[:], offs)
 
+        warm = sb.tile([P, 1], F32, name="warm")
+        nc.gpsimd.memset(warm[:], 0.0)
+
+        ident = sb.tile([P, P], F32, name="ident", align_bytes=64)
+        make_identity(nc, ident[:])
+
         scale_pool = sb.tile([P, T], U8, name="scale_pool", align_bytes=64)
         nc.sync.dma_start(
             scale_pool[96:128, :].bitcast(I32), k_scales.rearrange("o f t -> f o t").bitcast(I32)
         )
         nc.vector.memset(scale_pool[0:96, :].bitcast(I32), 0)
         lq_pool = sb.tile([P, T], F32, name="lq_pool", align_bytes=64)
-        nc.sync.dma_start(lq_pool[P - 1 : P, :], lq[0:1, :])
-        nc.vector.memset(lq_pool[0 : P - 1, :], 0.0)
+        nc.vector.memset(lq_pool[0 : P - 1, 0 : T // 2], 0.0)
+        nc.gpsimd.memset(lq_pool[0 : P - 1, T // 2 : T], 0.0)
 
-        word_pool = sb.tile([P, T], U32, name="word_pool", align_bytes=64)
-        nc.sync.dma_start(word_pool[:].bitcast(I32), k_words[0].rearrange("p t b -> p (t b)").bitcast(I32))
-        q_raw = []
-        for o in range(PASSES):
-            raw = sb.tile([P, PACK, NQ], F32, name="q_raw%d" % o, align_bytes=64)
-            nc.sync.dma_start(raw[:], qT[0, 512 * o : 512 * (o + 1), :].rearrange("(p t) w -> p t w", t=PACK))
-            q_raw.append(raw)
-
-        warm = sb.tile([P, 1], F32, name="warm")
-        nc.gpsimd.memset(warm[:], 0.0)
         nc.scalar.activation(warm[:], warm[:], ACT.Exp)
 
-        ident = sb.tile([P, P], F32, name="ident", align_bytes=64)
-        make_identity(nc, ident[:])
+        word_pool = sb.tile([P, T], U32, name="word_pool", align_bytes=64)
+        words_hbm = k_words[0].rearrange("p t b -> p (t b)").bitcast(I32)
+        nc.sync.dma_start(lq_pool[P - 1 : P, :], lq[0:1, :])
+        nc.sync.dma_start(word_pool[:].bitcast(I32), words_hbm)
+        order = [(0, 1), (1, 1), (0, 0), (1, 0)]
+        q_raw = {}
+        for o, h in order:
+            q_raw[o, h] = sb.tile([P, PACK, P], F32, name="q_raw%d%d" % (o, h), tag="q_raw%d%d" % (o, h), align_bytes=64)
+            nc.sync.dma_start(
+                q_raw[o, h][:],
+                qT[0, 512 * o : 512 * (o + 1), P * h : P * (h + 1)].rearrange("(p t) w -> p t w", t=PACK),
+            )
 
         k_scale = sb.tile([P, PASSES, N], U8, name="k_scale", align_bytes=64)
-        nc.gpsimd.memset(k_scale[:].rearrange("p o n -> p (o n)").bitcast(I32), 0)
+        nc.vector.memset(k_scale[:].rearrange("p o n -> p (o n)").bitcast(I32), 0)
 
         scale_listed = sb.tile([P, N], U8, name="scale_listed", align_bytes=64)
         nc.vector.tensor_copy(scale_listed[:], scale_pool[:].indirect(offsets[:]))
@@ -87,46 +93,51 @@ def tile_attend_nce_topk_kernel(tc, qT, k_words, k_scales, lq, offs, out):
                 scale_dealt[96 + 8 * quad : 96 + 8 * quad + 8, :].bitcast(I32),
             )
 
-        lq_listed = sb.tile([P, N], F32, name="lq_listed", align_bytes=64)
-        nc.vector.tensor_copy(lq_listed[:], lq_pool[:].indirect(offsets[:]))
-        lq_dealt = sb.tile([P, N], F32, name="lq_dealt", align_bytes=64)
-        nc.scalar.copy(
-            lq_dealt[:].rearrange("p (r j u) -> p r j u", r=TILES, j=RUNS),
-            lq_listed[:].rearrange("p (j r u) -> p r j u", r=TILES, j=RUNS),
-        )
-        lq_turned = bank(7, "lq_turned")
+        lq_dealt = sb.tile([P, TILES, RUNS, RUN_PART], F32, name="lq_dealt", align_bytes=64)
+        for a in range(2):
+            lq_listed = sb.tile([P, N // 2], F32, name="lq_listed%d" % a, tag="stage%d" % a, align_bytes=64)
+            nc.vector.tensor_copy(lq_listed[:], lq_pool[:].indirect(offsets[:, 16 * a : 16 * (a + 1)]))
+            nc.scalar.copy(
+                lq_dealt[:, :, RUNS // 2 * a : RUNS // 2 * (a + 1), :],
+                lq_listed[:].rearrange("p (j r u) -> p r j u", r=TILES, j=RUNS // 2),
+            )
+        lq_turned = bank(3, "lq_turned")
         for r in range(TILES):
-            nc.tensor.transpose(lq_turned[:, P * r : P * (r + 1)], lq_dealt[:, P * r : P * (r + 1)], ident[:])
+            nc.tensor.transpose(lq_turned[:, P * r : P * (r + 1)], lq_dealt[:, r].rearrange("p j u -> p (j u)"), ident[:])
         minus_lq = sb.tile([P, TILES], F32, name="minus_lq")
         minus_lq_cap = sb.tile([P, TILES], F32, name="minus_lq_cap")
         lq_columns = lq_turned[:].rearrange("p (r x) -> p r x", r=TILES)[:, :, P - 1]
         nc.scalar.activation(minus_lq[:], lq_columns, ACT.Copy, scale=-1.0)
-        nc.scalar.activation(minus_lq_cap[:], lq_columns, ACT.Copy, scale=-1.0, bias=-CAP)
+        nc.gpsimd.tensor_scalar(minus_lq_cap[:], minus_lq[:], 1.0, -CAP, ALU.mult, ALU.add)
 
-        word_listed = sb.tile([P, N], U32, name="word_listed", align_bytes=64)
-        nc.vector.tensor_copy(word_listed[:], word_pool[:].indirect(offsets[:]))
-        halves16 = word_listed[:].bitcast(U16).rearrange("p (j r u o) -> p o r j u", r=TILES, j=RUNS, o=PASSES)
-        k_codes = []
-        for o in range(PASSES):
-            codes = sb.tile([P, 2 * N], U8, name="k_codes%d" % o, align_bytes=64)
+        k_codes = sb.tile([P, PASSES, 2 * N], U8, name="k_codes", align_bytes=64)
+        codes16 = k_codes[:].rearrange("p o n -> p (o n)").bitcast(U16)
+        codes16 = codes16.rearrange("p (o r j u) -> p o r j u", o=PASSES, r=TILES, j=RUNS)
+        word_listed = []
+        for a in range(2):
+            listed = sb.tile([P, N // 2], U32, name="word_listed%d" % a, align_bytes=64)
+            nc.vector.tensor_copy(listed[:], word_pool[:].indirect(offsets[:, 16 * a : 16 * (a + 1)]))
+            word_listed.append(listed)
+        for a in range(2):
             nc.vector.tensor_copy(
-                codes[:].bitcast(U16).rearrange("p (r j u) -> p r j u", r=TILES, j=RUNS), halves16[:, o]
+                codes16[:, :, :, RUNS // 2 * a : RUNS // 2 * (a + 1), :],
+                word_listed[a][:].bitcast(U16).rearrange("p (j r u o) -> p o r j u", r=TILES, j=RUNS // 2, o=PASSES),
             )
-            k_codes.append(codes)
 
         q_codes = {}
         q_scale = {}
-        order = [(0, 0), (0, 1), (1, 1), (1, 0)]
         for o, h in order:
-            woven = sb.tile([P, P, PACK], BF16, name="q_woven%d%d" % (o, h), align_bytes=64)
+            woven = sb.tile(
+                [P, P, PACK], BF16, name="q_woven%d%d" % (o, h), tag="q_raw01" if (o, h) == (1, 0) else "stage%d" % o, align_bytes=64
+            )
             dst = woven[:].rearrange("p (c i) t -> p c t i", i=4)
-            src = q_raw[o][:, :, P * h : P * (h + 1)].rearrange("p t (c i) -> p c t i", i=4)
-            if (o, h) == (1, 1):
+            src = q_raw[o, h][:].rearrange("p t (c i) -> p c t i", i=4)
+            if (o, h) == (0, 0):
                 nc.vector.tensor_copy(dst, src)
             else:
                 nc.scalar.copy(dst, src)
             q_codes[o, h] = sb.tile([P, P], U32, name="q_codes%d%d" % (o, h), align_bytes=64)
-            q_scale[o, h] = sb.tile([P, P], U8, name="q_scale%d%d" % (o, h), align_bytes=64)
+            q_scale[o, h] = sb.tile([P, P], U8, name="q_scale%d%d" % (o, h), tag="stage1" if (o, h) == (0, 0) else "q_scale%d%d" % (o, h), align_bytes=64)
             nc.vector.quantize_mx(
                 out=q_codes[o, h][:].bitcast(FP8X4),
                 scales=q_scale[o, h][:],
@@ -141,7 +152,7 @@ def tile_attend_nce_topk_kernel(tc, qT, k_words, k_scales, lq, offs, out):
             for r in range(TILES):
                 nc.tensor.matmul_mx(
                     out=scores[r, h][:, 0:P],
-                    lhsT=k_codes[o][:, 2 * P * r : 2 * P * (r + 1)].bitcast(FP4X4),
+                    lhsT=k_codes[:, o, 2 * P * r : 2 * P * (r + 1)].bitcast(FP4X4),
                     lhsT_scale=k_scale[:, o, P * r : P * (r + 1)],
                     rhs=q_codes[o, h][:].bitcast(FP8X4),
                     rhs_scale=q_scale[o, h][:],
@@ -157,27 +168,34 @@ def tile_attend_nce_topk_kernel(tc, qT, k_words, k_scales, lq, offs, out):
             over[h] = sb.tile([P, TILES, P], F32, name="over%d" % h, align_bytes=64)
             for r in range(TILES):
                 nc.scalar.activation(expv[h][:, r, :], scores[r, h][:, 0:P], ACT.Exp, bias=minus_lq[:, r : r + 1])
+            if h == h_order[0]:
+                for r in (2, 3):
+                    nc.scalar.activation(
+                        over[h][:, r, :], scores[r, h][:, 0:P], ACT.Relu, bias=minus_lq_cap[:, r : r + 1]
+                    )
         terms = sb.tile([P, HALVES, RUNS, ROW], F32, name="terms", align_bytes=64)
         prod_turned = {}
+        quads = {}
         for n, h in enumerate(h_order):
-            for r in range(TILES):
+            grown = sb.tile([P, TILES, P], F32, name="grown%d" % h, align_bytes=64)
+            nc.vector.tensor_scalar(grown[:], expv[h][:], math.exp(CAP), 1.0, ALU.min, ALU.add)
+            for r in range(TILES) if n else (0, 1):
                 nc.vector.tensor_scalar(
                     over[h][:, r, :], scores[r, h][:, 0:P], minus_lq_cap[:, r : r + 1], 0.0, ALU.add, ALU.max
                 )
-            grown = sb.tile([P, TILES, P], F32, name="grown%d" % h, align_bytes=64)
-            nc.vector.tensor_scalar(grown[:], expv[h][:], math.exp(CAP), 1.0, ALU.min, ALU.add)
             pairs = sb.tile([P, 2, P], F32, name="pairs%d" % h, align_bytes=64)
             nc.vector.tensor_tensor(pairs[:], grown[:, 0:2, :], grown[:, 2:4, :], ALU.mult)
-            quads = sb.tile([P, P], F32, name="quads%d" % h, align_bytes=64)
-            nc.vector.tensor_tensor(quads[:], pairs[:, 0, :], pairs[:, 1, :], ALU.mult)
+            quads[h] = sb.tile([P, P], F32, name="quads%d" % h, align_bytes=64)
+            nc.vector.tensor_tensor(quads[h][:], pairs[:, 0, :], pairs[:, 1, :], ALU.mult)
+        for n, h in enumerate(h_order):
+            prod_turned[h] = bank(TILES * h_order[0] + 2 * n + 1, "prod_turned%d" % h)
+            nc.tensor.transpose(prod_turned[h][:, 0:P], quads[h][:], ident[:])
             over_sum = bank(TILES * h_order[0] + 2 * n, "over_sum%d" % h)
             for r in range(TILES):
                 nc.tensor.matmul(
                     over_sum[:, 0:P], over[h][:, r, :], ident[:],
                     start=(r == 0), stop=(r == TILES - 1), is_transpose=True,
                 )
-            prod_turned[h] = bank(TILES * h_order[0] + 2 * n + 1, "prod_turned%d" % h)
-            nc.tensor.transpose(prod_turned[h][:, 0:P], quads[:], ident[:])
             nc.vector.tensor_reduce(
                 terms[:, h, :, RUN_PART],
                 over_sum[:, 0:P].rearrange("p (j u) -> p j u", u=RUN_PART),

@@ -45,7 +45,6 @@ def tile_attend_nce_topk_kernel(tc, qT, k_words, k_scales, lq, offs, out):
             return ps.tile([P, 512], F32, name=name, tag="bank%d" % index)
 
         offsets = sb.tile([P, N // 16], U16, name="offsets")
-        nc.sync.dma_start(offsets[:], offs)
 
         warm = sb.tile([P, 1], F32, name="warm")
         nc.gpsimd.memset(warm[:], 0.0)
@@ -57,10 +56,10 @@ def tile_attend_nce_topk_kernel(tc, qT, k_words, k_scales, lq, offs, out):
         nc.sync.dma_start(
             scale_pool[96:128, :].bitcast(I32), k_scales.rearrange("o f t -> f o t").bitcast(I32)
         )
+        nc.sync.dma_start(offsets[:], offs)
         nc.vector.memset(scale_pool[0:96, :].bitcast(I32), 0)
         lq_pool = sb.tile([P, T], F32, name="lq_pool", align_bytes=64)
-        nc.vector.memset(lq_pool[0 : P - 1, 0 : T // 2], 0.0)
-        nc.gpsimd.memset(lq_pool[0 : P - 1, T // 2 : T], 0.0)
+        nc.vector.memset(lq_pool[0 : P - 1, :].bitcast(I32), 0)
 
         nc.scalar.activation(warm[:], warm[:], ACT.Exp)
 

@@ -177,15 +177,17 @@ def tile_attend_nce_topk_kernel(tc, qT, k_words, k_scales, lq, offs, out):
         quads = {}
         for n, h in enumerate(h_order):
             grown = sb.tile([P, TILES, P], F32, name="grown%d" % h, align_bytes=64)
-            nc.vector.tensor_scalar(grown[:], expv[h][:], math.exp(CAP), 1.0, ALU.min, ALU.add)
+            pairs = sb.tile([P, 2, P], F32, name="pairs%d" % h, align_bytes=64)
+            for a in range(2):
+                both = slice(2 * a, 2 * a + 2)
+                nc.vector.tensor_scalar(grown[:, both, :], expv[h][:, both, :], math.exp(CAP), 1.0, ALU.min, ALU.add)
+                nc.vector.tensor_tensor(pairs[:, a, :], grown[:, 2 * a, :], grown[:, 2 * a + 1, :], ALU.mult)
+            quads[h] = sb.tile([P, P], F32, name="quads%d" % h, align_bytes=64)
+            nc.vector.tensor_tensor(quads[h][:], pairs[:, 0, :], pairs[:, 1, :], ALU.mult)
             for r in range(TILES) if n else (0, 1):
                 nc.vector.tensor_scalar(
                     over[h][:, r, :], scores[r, h][:, 0:P], minus_lq_cap[:, r : r + 1], 0.0, ALU.add, ALU.max
                 )
-            pairs = sb.tile([P, 2, P], F32, name="pairs%d" % h, align_bytes=64)
-            nc.vector.tensor_tensor(pairs[:], grown[:, 0:2, :], grown[:, 2:4, :], ALU.mult)
-            quads[h] = sb.tile([P, P], F32, name="quads%d" % h, align_bytes=64)
-            nc.vector.tensor_tensor(quads[h][:], pairs[:, 0, :], pairs[:, 1, :], ALU.mult)
         for n, h in enumerate(h_order):
             prod_turned[h] = bank(TILES * h_order[0] + 2 * n + 1, "prod_turned%d" % h)
             nc.tensor.transpose(prod_turned[h][:, 0:P], quads[h][:], ident[:])

import math
from contextlib import ExitStack

import concourse.mybir as mybir
from concourse.masks import make_identity

F32 = mybir.dt.float32
BF16 = mybir.dt.bfloat16
I32 = mybir.dt.int32
U32 = mybir.dt.uint32
U16 = mybir.dt.uint16
U8 = mybir.dt.uint8
FP8X4 = mybir.dt.float8_e4m3fn_x4
FP4X4 = mybir.dt.float4_e2m1fn_x4
ACT = mybir.ActivationFunctionType
ALU = mybir.AluOpType
AXIS = mybir.AxisListType

P = 128
T = 2048
N = 512
D = 1024
NQ = 256
SEG = 32
PASSES = 2
PACK = 4
TILES = N // P
HALVES = NQ // P
RUNS = N // SEG
RUN_PART = SEG // TILES
CAP = 11.0
ROW = 12

FLOPS = 2 * NQ * N * D
BYTES = D * NQ * 4 + P * T * 4 + 2 * 16 * T + T * 4 + P * 32 * 2 + NQ * RUNS * 4


def tile_attend_nce_topk_kernel(tc, qT, k_words, k_scales, lq, offs, out):
    nc = tc.nc
    with ExitStack() as ctx:
        sb = ctx.enter_context(tc.tile_pool(name="sb", bufs=1))
        ps = ctx.enter_context(tc.psum_pool(name="ps", bufs=1))

        def bank(index, name):
            return ps.tile([P, 512], F32, name=name, tag="bank%d" % index)

        offsets = sb.tile([P, N // 16], U16, name="offsets")

        warm = sb.tile([P, 1], F32, name="warm")
        nc.gpsimd.memset(warm[:], 0.0)

        ident = sb.tile([P, P], F32, name="ident", align_bytes=64)
        make_identity(nc, ident[:])

        scale_pool = sb.tile([P, T], U8, name="scale_pool", align_bytes=64)
        nc.sync.dma_start(
            scale_pool[96:128, :].bitcast(I32), k_scales.rearrange("o f t -> f o t").bitcast(I32)
        )
        nc.sync.dma_start(offsets[:], offs)
        nc.vector.memset(scale_pool[0:96, :].bitcast(I32), 0)
        lq_pool = sb.tile([P, T], F32, name="lq_pool", align_bytes=64)
        nc.vector.memset(lq_pool[0 : P - 1, :].bitcast(I32), 0)

        nc.scalar.activation(warm[:], warm[:], ACT.Exp)

        word_pool = sb.tile([P, T], U32, name="word_pool", align_bytes=64)
        words_hbm = k_words[0].rearrange("p t b -> p (t b)").bitcast(I32)
        nc.sync.dma_start(lq_pool[P - 1 : P, :], lq[0:1, :])
        nc.sync.dma_start(word_pool[:].bitcast(I32), words_hbm)
        order = [(0, 1), (1, 1), (0, 0), (1, 0)]
        q_raw = {}
        for o, h in order:
            q_raw[o, h] = sb.tile([P, PACK, P], F32, name="q_raw%d%d" % (o, h), tag="q_raw%d%d" % (o, h), align_bytes=64)
            nc.sync.dma_start(
                q_raw[o, h][:],
                qT[0, 512 * o : 512 * (o + 1), P * h : P * (h + 1)].rearrange("(p t) w -> p t w", t=PACK),
            )

        k_scale = sb.tile([P, PASSES, N], U8, name="k_scale", align_bytes=64)
        nc.vector.memset(k_scale[:].rearrange("p o n -> p (o n)").bitcast(I32), 0)

        scale_listed = sb.tile([P, N], U8, name="scale_listed", align_bytes=64)
        nc.vector.tensor_copy(scale_listed[:], scale_pool[:].indirect(offsets[:]))
        scale_dealt = sb.tile([P, N], U8, name="scale_dealt", align_bytes=64)
        nc.vector.tensor_copy(
            scale_dealt[:].bitcast(I32).rearrange("p (r j u) -> p r j u", r=TILES, j=RUNS),
            scale_listed[:].bitcast(I32).rearrange("p (j r u) -> p r j u", r=TILES, j=RUNS),
        )
        for quad in range(4):
            nc.scalar.dma_start(
                k_scale[32 * quad : 32 * quad + 4].rearrange("p o n -> p (o n)").bitcast(I32),
                scale_dealt[96 + 8 * quad : 96 + 8 * quad + 8, :].bitcast(I32),
            )

        lq_dealt = sb.tile([P, TILES, RUNS, RUN_PART], F32, name="lq_dealt", align_bytes=64)
        for a in range(2):
            lq_listed = sb.tile([P, N // 2], F32, name="lq_listed%d" % a, tag="stage%d" % a, align_bytes=64)
            nc.vector.tensor_copy(lq_listed[:], lq_pool[:].indirect(offsets[:, 16 * a : 16 * (a + 1)]))
            nc.scalar.copy(
                lq_dealt[:, :, RUNS // 2 * a : RUNS // 2 * (a + 1), :],
                lq_listed[:].rearrange("p (j r u) -> p r j u", r=TILES, j=RUNS // 2),
            )
        lq_turned = bank(3, "lq_turned")
        for r in range(TILES):
            nc.tensor.transpose(lq_turned[:, P * r : P * (r + 1)], lq_dealt[:, r].rearrange("p j u -> p (j u)"), ident[:])
        minus_lq = sb.tile([P, TILES], F32, name="minus_lq")
        minus_lq_cap = sb.tile([P, TILES], F32, name="minus_lq_cap")
        lq_columns = lq_turned[:].rearrange("p (r x) -> p r x", r=TILES)[:, :, P - 1]
        nc.scalar.activation(minus_lq[:], lq_columns, ACT.Copy, scale=-1.0)
        nc.gpsimd.tensor_scalar(minus_lq_cap[:], minus_lq[:], 1.0, -CAP, ALU.mult, ALU.add)

        k_codes = sb.tile([P, PASSES, 2 * N], U8, name="k_codes", align_bytes=64)
        codes16 = k_codes[:].rearrange("p o n -> p (o n)").bitcast(U16)
        codes16 = codes16.rearrange("p (o r j u) -> p o r j u", o=PASSES, r=TILES, j=RUNS)
        word_listed = []
        for a in range(2):
            listed = sb.tile([P, N // 2], U32, name="word_listed%d" % a, align_bytes=64)
            nc.vector.tensor_copy(listed[:], word_pool[:].indirect(offsets[:, 16 * a : 16 * (a + 1)]))
            word_listed.append(listed)
        for a in range(2):
            nc.vector.tensor_copy(
                codes16[:, :, :, RUNS // 2 * a : RUNS // 2 * (a + 1), :],
                word_listed[a][:].bitcast(U16).rearrange("p (j r u o) -> p o r j u", r=TILES, j=RUNS // 2, o=PASSES),
            )

        q_codes = {}
        q_scale = {}
        for o, h in order:
            woven = sb.tile(
                [P, P, PACK], BF16, name="q_woven%d%d" % (o, h), tag="q_raw01" if (o, h) == (1, 0) else "stage%d" % o, align_bytes=64
            )
            dst = woven[:].rearrange("p (c i) t -> p c t i", i=4)
            src = q_raw[o, h][:].rearrange("p t (c i) -> p c t i", i=4)
            if (o, h) == (0, 0):
                nc.vector.tensor_copy(dst, src)
            else:
                nc.scalar.copy(dst, src)
            q_codes[o, h] = sb.tile([P, P], U32, name="q_codes%d%d" % (o, h), align_bytes=64)
            q_scale[o, h] = sb.tile([P, P], U8, name="q_scale%d%d" % (o, h), tag="stage1" if (o, h) == (0, 0) else "q_scale%d%d" % (o, h), align_bytes=64)
            nc.vector.quantize_mx(
                out=q_codes[o, h][:].bitcast(FP8X4),
                scales=q_scale[o, h][:],
                in_=woven[:].rearrange("p w t -> p (w t)"),
            )

        scores = {}
        for h in range(HALVES):
            for r in range(TILES):
                scores[r, h] = bank(TILES * h + r, "scores%d%d" % (r, h))
        for o, h in order:
            for r in range(TILES):
                nc.tensor.matmul_mx(
                    out=scores[r, h][:, 0:P],
                    lhsT=k_codes[:, o, 2 * P * r : 2 * P * (r + 1)].bitcast(FP4X4),
                    lhsT_scale=k_scale[:, o, P * r : P * (r + 1)],
                    rhs=q_codes[o, h][:].bitcast(FP8X4),
                    rhs_scale=q_scale[o, h][:],
                    start=(o == 0),
                    stop=(o == PASSES - 1),
                )

        h_order = [1, 0]
        expv = {}
        over = {}
        for h in h_order:
            expv[h] = sb.tile([P, TILES, P], F32, name="expv%d" % h, align_bytes=64)
            over[h] = sb.tile([P, TILES, P], F32, name="over%d" % h, align_bytes=64)
            for r in range(TILES):
                nc.scalar.activation(expv[h][:, r, :], scores[r, h][:, 0:P], ACT.Exp, bias=minus_lq[:, r : r + 1])
            if h == h_order[0]:
                for r in (2, 3):
                    nc.scalar.activation(
                        over[h][:, r, :], scores[r, h][:, 0:P], ACT.Relu, bias=minus_lq_cap[:, r : r + 1]
                    )
        terms = sb.tile([P, HALVES, RUNS, ROW], F32, name="terms", align_bytes=64)
        prod_turned = {}
        quads = {}
        for n, h in enumerate(h_order):
            grown = sb.tile([P, TILES, P], F32, name="grown%d" % h, align_bytes=64)
            pairs = sb.tile([P, 2, P], F32, name="pairs%d" % h, align_bytes=64)
            for a in range(2):
                both = slice(2 * a, 2 * a + 2)
                nc.vector.tensor_scalar(grown[:, both, :], expv[h][:, both, :], math.exp(CAP), 1.0, ALU.min, ALU.add)
                nc.vector.tensor_tensor(pairs[:, a, :], grown[:, 2 * a, :], grown[:, 2 * a + 1, :], ALU.mult)
            quads[h] = sb.tile([P, P], F32, name="quads%d" % h, align_bytes=64)
            nc.vector.tensor_tensor(quads[h][:], pairs[:, 0, :], pairs[:, 1, :], ALU.mult)
            for r in range(TILES) if n else (0, 1):
                nc.vector.tensor_scalar(
                    over[h][:, r, :], scores[r, h][:, 0:P], minus_lq_cap[:, r : r + 1], 0.0, ALU.add, ALU.max
                )
        for n, h in enumerate(h_order):
            prod_turned[h] = bank(TILES * h_order[0] + 2 * n + 1, "prod_turned%d" % h)
            nc.tensor.transpose(prod_turned[h][:, 0:P], quads[h][:], ident[:])
            over_sum = bank(TILES * h_order[0] + 2 * n, "over_sum%d" % h)
            for r in range(TILES):
                nc.tensor.matmul(
                    over_sum[:, 0:P], over[h][:, r, :], ident[:],
                    start=(r == 0), stop=(r == TILES - 1), is_transpose=True,
                )
            nc.vector.tensor_reduce(
                terms[:, h, :, RUN_PART],
                over_sum[:, 0:P].rearrange("p (j u) -> p j u", u=RUN_PART),
                AXIS.X,
                ALU.add,
            )
        result = sb.tile([P, HALVES, RUNS], F32, name="result", align_bytes=64)
        for h in h_order:
            nc.scalar.activation(
                terms[:, h, :, 0:RUN_PART],
                prod_turned[h][:, 0:P].rearrange("p (j u) -> p j u", u=RUN_PART),
                ACT.Ln,
            )
            nc.vector.tensor_reduce(result[:, h, :], terms[:, h, :, 0 : RUN_PART + 1], AXIS.X, ALU.add)
        nc.sync.dma_start(out[0].rearrange("(h p) j -> p h j", p=P), result[:])
